import numpy as np
import ml_dtypes


def mxq(x, axis, fmt="e4m3"):
    dtype, down = {"e4m3": (ml_dtypes.float8_e4m3fn, 7), "e5m2": (ml_dtypes.float8_e5m2, 14)}[fmt]
    v = np.moveaxis(np.asarray(x, np.float32).astype(ml_dtypes.bfloat16).astype(np.float64), axis, -1)
    blocks = v.reshape(v.shape[:-1] + (-1, 32))
    amax = np.abs(blocks).max(-1, keepdims=True)
    byte = np.maximum(np.where(amax > 0, np.frexp(amax)[1] - 1 + 127, 0) - down, 1)
    scale = np.exp2(byte - 127.0)
    codes = (blocks / scale).astype(np.float32).astype(dtype).astype(np.float64)
    return np.moveaxis((codes * scale).reshape(v.shape), -1, axis)


WIDE = False


def mx_kscale(k):
    if not WIDE:
        return np.ones(k)
    levels = np.array([10, -10, 5, -5, 0])
    if k % 512:
        return np.exp2(np.random.permutation(np.resize(levels, k // 32))).repeat(32)
    a = np.empty((k // 512, 16))
    for p in range(k // 512):
        a[p, :8] = np.random.permutation(np.resize(levels, 8))
        for g in range(8):
            far = levels[np.abs(levels - a[p, g]) >= 10]
            a[p, g + 8] = far[np.random.randint(len(far))]
    return np.exp2(a.ravel()).repeat(32)


BF16 = ml_dtypes.bfloat16


def bf(x):
    return np.asarray(x, np.float32).astype(BF16)


def f64(x):
    return np.asarray(x).astype(np.float64)


E2M1 = np.array([0.0, 0.5, 1.0, 1.5, 2.0, 3.0, 4.0, 6.0, -0.0, -0.5, -1.0, -1.5, -2.0, -3.0, -4.0, -6.0])


def pack_weight(w, fmt):
    k, n = w.shape
    w = f64(bf(w)).reshape(k // 32, 32, n)
    amax = np.abs(w).max(1)
    if fmt == "e4m3":
        byte = np.frexp(amax)[1] - 1 + 127 - 7
    else:
        mant, ex = np.frexp(amax / 6.0)
        byte = np.where(mant > 0.5, ex, ex - 1) + 127
    byte = np.clip(np.where(amax > 0, byte, 1), 1, 254)
    scaled = (w * np.exp2(127.0 - byte)[:, None, :]).reshape(k, n).astype(np.float32)
    by_word = np.ascontiguousarray(scaled.reshape(k // 512, 128, 4, n).transpose(0, 1, 3, 2))
    if fmt == "e4m3":
        words = by_word.astype(ml_dtypes.float8_e4m3fn).view(np.uint8)
    else:
        c = by_word.astype(ml_dtypes.float4_e2m1fn).view(np.uint8) & 0xF
        words = c[..., 0::2] | (c[..., 1::2] << 4)
    return np.ascontiguousarray(words), np.ascontiguousarray(byte.astype(np.uint8).reshape(k // 512, 16, n))


def unpack_weight(words, scales, fmt):
    g, p, n, _ = words.shape
    if fmt == "e4m3":
        vals = np.ascontiguousarray(words).view(ml_dtypes.float8_e4m3fn).astype(np.float64)
    else:
        nib = np.empty((g, p, n, 4), np.uint8)
        nib[..., 0::2] = words & 0xF
        nib[..., 1::2] = words >> 4
        vals = E2M1[nib]
    vals = vals * np.repeat(np.exp2(scales.astype(np.float64) - 127.0), 8, axis=1)[..., None]
    return vals.transpose(0, 1, 3, 2).reshape(g * 512, n)
def pack4(w):
    words, scales = pack_weight(w, "e2m1")
    return words.reshape(words.shape[0], 128, -1), scales


def unpack4(words, scales):
    return unpack_weight(words.reshape(words.shape[0], 128, -1, 2), scales, "e2m1")


def planes(Y):
    n, m = Y.shape
    b = f64(bf(Y)).reshape(n // 32, 32, m)
    amax = np.abs(b).max(1)
    byte = np.clip(np.where(amax > 0, np.frexp(amax)[1] - 1 + 127 - 7, 1), 1, 254)
    codes = (b * np.exp2(127.0 - byte)[:, None, :]).reshape(n, m).astype(np.float32).astype(ml_dtypes.float8_e4m3fn).view(np.uint8)
    words = codes.reshape(n // 512, 128, 4, m).transpose(0, 1, 3, 2)
    return np.ascontiguousarray(words), np.ascontiguousarray(byte.astype(np.uint8).reshape(n // 512, 16, m))


B, HH, WW, D, F, KH, KW = 1, 32, 32, 512, 1024, 3, 3
F2 = 2 * F


def silu(z):
    return z / (1.0 + np.exp(-z))


def depthwise_corr(u, wd):
    rows, cols = u.shape[1], u.shape[2]
    ph, pw = KH // 2, KW // 2
    upad = np.pad(u, ((0, 0), (ph, ph), (pw, pw), (0, 0)))
    c = np.zeros_like(u)
    for r in range(KH):
        band = upad[:, r:r + rows, :, :]
        for t in range(KW):
            c = c + wd[r, t] * band[:, :, t:t + cols, :]
    return c


def setup_inputs():
    s, t = mx_kscale(D), mx_kscale(F)
    x = bf(np.random.standard_normal((B, HH, WW, D)) * s)
    w1_words, w1_scales = pack4(np.random.standard_normal((D, F2)) / np.sqrt(D) / s[:, None])
    b1 = bf(np.random.standard_normal(F2) * 0.3)
    wd = bf(np.random.standard_normal((KH, KW, F2)) * 0.5)
    gain = bf((1.0 + 0.1 * np.random.standard_normal(F)) * t)
    w2_words, w2_scales = pack4(np.random.standard_normal((F, D)) * 2.0 / np.sqrt(F) / t[:, None])
    return {"x": x,
            "w1_words": w1_words,
            "w1_scales": w1_scales,
            "b1": b1,
            "wd": wd,
            "gain": gain,
            "w2_words": w2_words,
            "w2_scales": w2_scales}


def core(x, w1_words, w1_scales, b1, wd, gain, w2_words, w2_scales):
    f = gain.shape[0]
    h = (mxq(f64(x), 3, "e4m3") @ unpack4(w1_words, w1_scales)) + f64(b1)
    u = silu(h)
    c = depthwise_corr(u, f64(wd))
    ca = c[..., :f]
    cb = c[..., f:]
    g = f64(gain) * ca * silu(cb)
    return mxq(g, 3, "e4m3") @ unpack4(w2_words, w2_scales)


def reference(x, w1_words, w1_scales, b1, wd, gain, w2_words, w2_scales):
    R_out = core(x, w1_words, w1_scales, b1, wd, gain, w2_words, w2_scales)
    words, scales = planes(np.moveaxis(R_out, 3, 0).reshape(512, -1))
    return R_out, words, scales

@@ -1,0 +1,384 @@
+from contextlib import ExitStack
+
+import concourse.mybir as mybir
+from concourse.masks import make_identity
+
+F32 = mybir.dt.float32
+BF16 = mybir.dt.bfloat16
+I32 = mybir.dt.int32
+U32 = mybir.dt.uint32
+U8 = mybir.dt.uint8
+FP8X4 = mybir.dt.float8_e4m3fn_x4
+FP4X4 = mybir.dt.float4_e2m1fn_x4
+ACT = mybir.ActivationFunctionType
+ALU = mybir.AluOpType
+
+P = 128
+GRID = 32
+TOK = GRID * GRID
+D = 512
+F = 1024
+F2 = 2 * F
+CHUNKS = F2 // P
+PAIRS = F // P
+TILES = TOK // P
+BANK = 512
+PITCH = 36
+LEAD = 4
+U_LEN = LEAD + PITCH * (GRID + 2) + LEAD
+U_BUFS = 4
+
+FLOPS = 2 * TOK * D * F2 + 2 * TOK * F * D + 2 * 9 * TOK * F2
+
+
+def tile_sanamixffndepthwiseglu_x2_kernel(
+    tc, x, w1_words, w1_scales, b1, wd, gain, w2_words, w2_scales, out_0, out_1, out_2
+):
+    nc = tc.nc
+    x_rows = x.rearrange("b i j k -> (b i j) k").rearrange("(q p) k -> p q k", p=P)
+    out_rows = out_0.rearrange("b i j d -> (b i j) d")
+    out_words = out_1.rearrange("g p m t -> p (g m t)").bitcast(I32)
+    wd_rows = wd.rearrange("r t (m c) -> (r t m) c", c=P)
+
+    with ExitStack() as ctx:
+        keep = ctx.enter_context(tc.tile_pool(name="keep", bufs=1))
+        prods = ctx.enter_context(tc.tile_pool(name="prods", bufs=14))
+        gates = ctx.enter_context(tc.tile_pool(name="gates", bufs=4))
+        outs = ctx.enter_context(tc.tile_pool(name="outs", bufs=4))
+        psum = ctx.enter_context(tc.psum_pool(name="psum", bufs=1))
+        ctx.enter_context(tc.manual_schedule())
+
+        def bank(index, shape, dtype=F32):
+            return psum.tile(shape, dtype, name="bank%d" % index, tag="bank%d" % index)
+
+        xs = [keep.tile([P, TILES // 2, D], BF16, name="xs%d" % h, align_bytes=64) for h in range(2)]
+        w1w = [keep.tile([P, F2], U8, name="w1w%d" % h, align_bytes=64) for h in range(2)]
+        w1s = keep.tile([P, F2], U8, align_bytes=64)
+        w2w = keep.tile([P, 2, 2 * D], U8, align_bytes=64)
+        w2s = keep.tile([P, 2, D], U8, align_bytes=64)
+        rows_a = keep.tile([P, P], BF16, align_bytes=64)
+        rows_b = keep.tile([P, P], BF16, align_bytes=64)
+        cols = keep.tile([P, 2 * P], F32, align_bytes=64)
+        ident = keep.tile([P, P], F32, align_bytes=64)
+        ident_bf = keep.tile([P, P], BF16, align_bytes=64)
+        perm = keep.tile([P, P], F32, align_bytes=64)
+        zeros = keep.tile([P, LEAD + PITCH], F32, align_bytes=64)
+        u = [keep.tile([P, U_LEN], F32, name="u%d" % i, align_bytes=64) for i in range(U_BUFS)]
+        xg = keep.tile([P, TOK, 4], BF16, align_bytes=64)
+        xc = keep.tile([P, TOK], U32, align_bytes=64)
+        xsc = keep.tile([P, TOK], U8, align_bytes=64)
+        gt = keep.tile([P, TILES, 2, 2, 2 * P], BF16, align_bytes=64)
+        gg = keep.tile([P, 2, TOK, 4], BF16, align_bytes=64)
+        gc = keep.tile([P, 2, TOK], U32, align_bytes=64)
+        gsc = keep.tile([P, 2, TOK], U8, align_bytes=64)
+        og = keep.tile([P, TOK, 4], BF16, align_bytes=64)
+        oc = keep.tile([P, TOK], U32, align_bytes=64)
+        osc = keep.tile([P, TOK], U8, align_bytes=64)
+
+        nc.scalar.dma_start(out=xs[0][:], in_=x_rows[:, 0:4, :])
+        nc.vector.memset(zeros[:], 0.0)
+        nc.vector.memset(w1s[:].bitcast(U32), 0)
+        nc.vector.memset(rows_b[:], 0.0)
+        nc.scalar.activation(out=u[0][:, 0 : LEAD + PITCH], in_=zeros[:], func=ACT.Silu)
+        make_identity(nc, ident[:])
+        nc.sync.dma_start(out=xs[1][:], in_=x_rows[:, 4:8, :])
+        nc.sync.dma_start(out=w1w[1][:].bitcast(I32), in_=w1_words[0, :, F2 : 2 * F2].bitcast(I32))
+        nc.sync.dma_start(out=rows_b[16:32, :], in_=b1.rearrange("(m c) -> m c", c=P))
+        nc.sync.dma_start(out=rows_b[0:16, :], in_=wd_rows[P : P + 16, :])
+        nc.sync.dma_start(out=rows_b[32:40, :], in_=gain.rearrange("(m c) -> m c", c=P))
+        for quad in range(4):
+            nc.sync.dma_start(
+                out=w1s[32 * quad : 32 * quad + 4, :].bitcast(I32),
+                in_=w1_scales[0, 4 * quad : 4 * quad + 4, :].bitcast(I32),
+            )
+        nc.sync.dma_start(out=rows_a[:], in_=wd_rows[0:P, :])
+        nc.sync.dma_start(out=w1w[0][:].bitcast(I32), in_=w1_words[0, :, 0:F2].bitcast(I32))
+
+        nc.vector.tensor_copy(out=ident_bf[:], in_=ident[:])
+        nc.vector.tensor_copy(
+            out=perm[:].rearrange("p (u c e) -> p u c e", u=2, e=2),
+            in_=ident[:].rearrange("p (c u e) -> p u c e", u=2, e=2),
+        )
+        nc.vector.memset(u[0][:, LEAD + PITCH :], 0.0)
+        for i in range(1, U_BUFS):
+            nc.vector.memset(u[i][:], 0.0)
+        nc.vector.memset(w2s[:].rearrange("p g n -> p (g n)").bitcast(U32), 0)
+        nc.sync.dma_start(out=w2w[:].bitcast(I32), in_=w2_words.rearrange("g p n -> p g n").bitcast(I32))
+        for quad in range(4):
+            nc.sync.dma_start(
+                out=w2s[32 * quad : 32 * quad + 4, :, :].bitcast(I32),
+                in_=w2_scales[:, 4 * quad : 4 * quad + 4, :].rearrange("g r n -> r g n").bitcast(I32),
+            )
+
+        def turn_words(index, sources):
+            pt = bank(index, [P, 2, 2, P])
+            for qq in range(2):
+                for half in range(2):
+                    nc.tensor.transpose(pt[:, qq, half, :], sources[qq][half], ident[:])
+            return pt
+
+        def weave(engine, grouped, pt):
+            dst = grouped.bitcast(F32).rearrange("p (q r) u -> p q r u", q=2)
+            src = pt[:].rearrange("p q u r -> p q r u")
+            if engine == "scalar":
+                nc.scalar.copy(out=dst, in_=src)
+            else:
+                nc.vector.tensor_copy(out=dst, in_=src)
+
+        def quantize(grouped, codes, scales):
+            nc.vector.quantize_mx(out=codes.bitcast(FP8X4), scales=scales, in_=grouped.rearrange("p r t -> p (r t)"))
+
+        def x_sources(r):
+            res = []
+            for qq in range(2):
+                q = 2 * r + qq
+                words = xs[q // 4][:, q % 4, :].bitcast(F32)
+                res.append([words[:, half : 2 * P : 2] for half in range(2)])
+            return res
+
+        order = [c for j in range(PAIRS) for c in (PAIRS + j, j)]
+        hbank = {}
+
+        def expand(s, h):
+            c = order[s]
+            hb = bank(2 * (s % 2) + h, [P, BANK])
+            hbank[s, h] = hb
+            w = w1w[c // PAIRS]
+            off = 2 * P * (c % PAIRS)
+            nc.tensor.matmul_mx(
+                out=hb[:],
+                lhsT=w[:, off : off + 2 * P].bitcast(FP4X4),
+                lhsT_scale=w1s[:, P * c : P * (c + 1)],
+                rhs=xc[:, BANK * h : BANK * (h + 1)].bitcast(FP8X4),
+                rhs_scale=xsc[:, BANK * h : BANK * (h + 1)],
+                start=True,
+                stop=True,
+            )
+
+        def window(s, r, t):
+            first = LEAD + PITCH * r + t - 1
+            return u[s % U_BUFS][:, first : first + PITCH * GRID].rearrange("p (i j) -> p i j", j=PITCH)[:, :, 0:GRID]
+
+        def activate(s, h):
+            c = order[s]
+            half_rows = GRID // 2
+            nc.scalar.activation(
+                out=window(s, 1, 1)[:, half_rows * h : half_rows * (h + 1), :],
+                in_=hbank[s, h][:].rearrange("p (i j) -> p i j", j=GRID),
+                func=ACT.Silu,
+                bias=cols[:, 9 * CHUNKS + c : 9 * CHUNKS + c + 1],
+            )
+
+        def weight(s, tap):
+            col = CHUNKS * tap + order[s]
+            return cols[:, col : col + 1]
+
+        def product(engine, s, tap):
+            pr = prods.tile([P, TOK], F32, name="pr", tag="pr")
+            dst = pr[:].rearrange("p (i j) -> p i j", j=GRID)
+            src = window(s, tap // 3, tap % 3)
+            if engine == "scalar":
+                nc.scalar.activation(out=dst, in_=src, func=ACT.Copy, scale=weight(s, tap))
+            else:
+                nc.vector.tensor_scalar(out=dst, in0=src, scalar1=weight(s, tap), scalar2=None, op0=ALU.mult)
+            return pr
+
+        def add_product(s, tap, pr):
+            dst = pr[:].rearrange("p (i j) -> p i j", j=GRID)
+            nc.vector.scalar_tensor_tensor(
+                out=dst, in0=window(s, tap // 3, tap % 3), scalar=weight(s, tap), in1=dst, op0=ALU.mult, op1=ALU.add
+            )
+
+        cbank = {}
+
+        def accumulate(s, pr, first, last):
+            for h in range(2):
+                if first:
+                    cbank[s, h] = bank(4 + 2 * (s % 2) + h, [P, 4, P])
+                for qq in range(4):
+                    q = 4 * h + qq
+                    nc.tensor.matmul(
+                        out=cbank[s, h][:, qq, :],
+                        lhsT=pr[:, P * q : P * (q + 1)],
+                        rhs=perm[:],
+                        is_transpose=True,
+                        start=(first and qq == 0),
+                        stop=(last and qq == 3),
+                    )
+
+        gate = {}
+
+        def gate_silu(s, h):
+            gate[h] = gates.tile([P, 4, P], F32, name="gate", tag="gate")
+            nc.scalar.activation(out=gate[h][:], in_=cbank[s, h][:], func=ACT.Silu)
+
+        def gate_mul(s, h):
+            j = order[s]
+            nc.vector.tensor_tensor(
+                out=gt[:, 4 * h : 4 * h + 4, j // 4, :, 64 * (j % 4) : 64 * (j % 4 + 1)],
+                in0=cbank[s, h][:].rearrange("p q (u c) -> p q u c", u=2),
+                in1=gate[h][:].rearrange("p q (u c) -> p q u c", u=2),
+                op=ALU.mult,
+            )
+
+        def g_sources(group, r):
+            return [[gt[:, 2 * r + qq, group, half, :].bitcast(F32) for half in range(2)] for qq in range(2)]
+
+        xt = [turn_words(4 + r, x_sources(r)) for r in range(2)]
+        ct = bank(3, [P, 2, P], BF16)
+        nc.tensor.transpose(ct[:, 1, :], rows_b[:], ident_bf[:])
+        nc.tensor.transpose(ct[:, 0, :], rows_a[:], ident_bf[:])
+        xt += [turn_words(4 + r, x_sources(r)) for r in range(2, 4)]
+        weave("vector", xg[:, 0:256, :], xt[0])
+        weave("scalar", xg[:, 256:512, :], xt[1])
+        nc.vector.tensor_copy(out=cols[:], in_=ct[:].rearrange("p a c -> p (a c)"))
+        quantize(xg[:, 0:512, :], xc[:, 0:512], xsc[:, 0:512])
+        weave("scalar", xg[:, 768:1024, :], xt[3])
+        weave("vector", xg[:, 512:768, :], xt[2])
+        taps = cols[:, 0 : 9 * CHUNKS].rearrange("p (k m) -> p k m", m=CHUNKS)[:, :, 0:PAIRS]
+        nc.vector.tensor_tensor(
+            out=taps,
+            in0=taps,
+            in1=cols[:, 10 * CHUNKS : 10 * CHUNKS + PAIRS].unsqueeze(1).to_broadcast([P, 9, PAIRS]),
+            op=ALU.mult,
+        )
+        quantize(xg[:, 512:1024, :], xc[:, 512:1024], xsc[:, 512:1024])
+        expand(0, 0)
+        expand(1, 0)
+        expand(0, 1)
+        expand(1, 1)
+        activate(0, 0)
+        activate(0, 1)
+
+        gpt = {}
+        for s in range(CHUNKS):
+            p1 = product("scalar", s, 0)
+            pa = product("vector", s, 1)
+            pc = product("vector", s, 4)
+            accumulate(s, pc, True, False)
+            accumulate(s, p1, False, False)
+            if s + 1 < CHUNKS:
+                activate(s + 1, 0)
+                activate(s + 1, 1)
+            if s in (10, 12):
+                for k in range(2):
+                    r = s - 10 + k
+                    weave("scalar", gg[:, 0, 256 * r : 256 * (r + 1), :], gpt[r])
+            pb = product("vector", s, 7)
+            pd = product("vector", s, 3)
+            p2 = product("scalar", s, 2)
+            accumulate(s, pd, False, False)
+            accumulate(s, p2, False, False)
+            if s % 2 == 1:
+                gate_silu(s - 1, 0)
+                gate_silu(s - 1, 1)
+            elif s > 0:
+                gate_mul(s - 1, 0)
+                gate_mul(s - 1, 1)
+            if s in (11, 13):
+                lo = 512 * ((s - 11) // 2)
+                quantize(gg[:, 0, lo : lo + 512, :], gc[:, 0, lo : lo + 512], gsc[:, 0, lo : lo + 512])
+            add_product(s, 5, pa)
+            p3 = product("scalar", s, 6)
+            accumulate(s, pa, False, False)
+            add_product(s, 8, pb)
+            accumulate(s, p3, False, False)
+            accumulate(s, pb, False, True)
+            if s % 2 == 0 and s + 2 < CHUNKS:
+                for k in (2, 3):
+                    expand(s + k, 0)
+                    expand(s + k, 1)
+            if s in (9, 11):
+                for k in range(2):
+                    r = s - 9 + k
+                    gpt[r] = turn_words(k, g_sources(0, r))
+
+        last = CHUNKS - 1
+        o32 = {}
+        ob = {}
+        acc = {}
+        opt = {}
+
+        def g_turn(r):
+            gpt[r] = turn_words((4, 5, 6, 7)[r], g_sources(1, r))
+
+        def g_weave(r):
+            weave("scalar", gg[:, 1, 256 * r : 256 * (r + 1), :], gpt[r])
+
+        def g_quant(r):
+            cs = slice(256 * r, 256 * (r + 1))
+            quantize(gg[:, 1, cs, :], gc[:, 1, cs], gsc[:, 1, cs])
+
+        def project(q):
+            acc[q] = bank(q % 4, [P, D])
+            for group in range(2):
+                nc.tensor.matmul_mx(
+                    out=acc[q][:],
+                    lhsT=gc[:, group, P * q : P * (q + 1)].bitcast(FP8X4),
+                    lhsT_scale=gsc[:, group, P * q : P * (q + 1)],
+                    rhs=w2w[:, group, :].bitcast(FP4X4),
+                    rhs_scale=w2s[:, group, :],
+                    start=(group == 0),
+                    stop=(group == 1),
+                )
+
+        def evacuate(q):
+            o32[q] = outs.tile([P, D], F32, name="o32", tag="o32")
+            nc.scalar.copy(out=o32[q][:], in_=acc[q][:])
+            nc.sync.dma_start(out=out_rows[P * q : P * (q + 1), :], in_=o32[q][:])
+
+        def narrow(q):
+            ob[q] = outs.tile([P, 2, 2 * P], BF16, name="ob", tag="ob")
+            nc.vector.tensor_copy(
+                out=ob[q][:].rearrange("p u (c e) -> p u c e", e=2),
+                in_=o32[q][:].rearrange("p (c u e) -> p u c e", u=2, e=2),
+            )
+
+        def o_turn(r):
+            opt[r] = turn_words(4 + r, [[ob[2 * r + qq][:, half, :].bitcast(F32) for half in range(2)] for qq in range(2)])
+
+        def o_weave(r):
+            weave("vector", og[:, 256 * r : 256 * (r + 1), :], opt[r])
+
+        def o_quant(r):
+            cs = slice(256 * r, 256 * (r + 1))
+            quantize(og[:, cs, :], oc[:, cs], osc[:, cs])
+            nc.sync.dma_start(out=out_words[:, cs], in_=oc[:, cs].bitcast(I32))
+
+        gate_mul(last, 0)
+        g_turn(0)
+        g_turn(1)
+        gate_mul(last, 1)
+        g_weave(0)
+        g_weave(1)
+        g_turn(2)
+        g_turn(3)
+        g_quant(0)
+        g_quant(1)
+        for q in range(4):
+            project(q)
+        g_weave(2)
+        g_weave(3)
+        g_quant(2)
+        g_quant(3)
+        for r in range(4):
+            evacuate(2 * r)
+            evacuate(2 * r + 1)
+            if r < 2:
+                project(2 * r + 4)
+                project(2 * r + 5)
+            narrow(2 * r)
+            narrow(2 * r + 1)
+            if r > 0:
+                o_weave(r - 1)
+            if r > 1:
+                o_quant(r - 2)
+            o_turn(r)
+        o_quant(2)
+        o_weave(3)
+        o_quant(3)
+        for quad in range(4):
+            nc.sync.dma_start(
+                out=out_2[0, 4 * quad : 4 * quad + 4, :].bitcast(I32),
+                in_=osc[32 * quad : 32 * quad + 4, :].bitcast(I32),
+            )

@@ -19,40 +19,58 @@ TOK = GRID * GRID
 D = 512
 F = 1024
 F2 = 2 * F
+TAPS = 9
 CHUNKS = F2 // P
 PAIRS = F // P
 TILES = TOK // P
-BANK = 512
-PITCH = 36
-LEAD = 4
-U_LEN = LEAD + PITCH * (GRID + 2) + LEAD
-U_BUFS = 4
+ROWS = P // GRID
+HALF = TOK // 2
+BANK_TILES = 4
+QUADS = 4
+W1_BYTES = 2 * P
 
-FLOPS = 2 * TOK * D * F2 + 2 * TOK * F * D + 2 * 9 * TOK * F2
+LEAD = 4
+PITCH = GRID + LEAD
+U_LEN = PITCH * (GRID + 2)
+
+U_BUFS = 4
+TOP_BUFS = 6
+PROD_BUFS = 9
+GATE_BUFS = 4
+OUT_BUFS = 4
+
+BIAS_COL = TAPS * CHUNKS
+GAIN_COL = BIAS_COL + CHUNKS
+
+SUM_BANK = 4
+
+FLOPS = 2 * TOK * D * F2 + 2 * TOK * F * D + 2 * TAPS * TOK * F2
 
 
 def tile_sanamixffndepthwiseglu_x2_kernel(
     tc, x, w1_words, w1_scales, b1, wd, gain, w2_words, w2_scales, out_0, out_1, out_2
 ):
     nc = tc.nc
-    x_rows = x.rearrange("b i j k -> (b i j) k").rearrange("(q p) k -> p q k", p=P)
+    x_tiles = x.rearrange("b i j k -> (b i j) k").rearrange("(q p) k -> p q k", p=P)
     out_rows = out_0.rearrange("b i j d -> (b i j) d")
     out_words = out_1.rearrange("g p m t -> p (g m t)").bitcast(I32)
     wd_rows = wd.rearrange("r t (m c) -> (r t m) c", c=P)
+    w1_branches = w1_words.rearrange("g p (a n) -> p (g a) n", a=2)
 
     with ExitStack() as ctx:
         keep = ctx.enter_context(tc.tile_pool(name="keep", bufs=1))
-        prods = ctx.enter_context(tc.tile_pool(name="prods", bufs=14))
-        gates = ctx.enter_context(tc.tile_pool(name="gates", bufs=4))
-        outs = ctx.enter_context(tc.tile_pool(name="outs", bufs=4))
+        prods = ctx.enter_context(tc.tile_pool(name="prods", bufs=PROD_BUFS))
+        gates = ctx.enter_context(tc.tile_pool(name="gates", bufs=GATE_BUFS))
+        outs = ctx.enter_context(tc.tile_pool(name="outs", bufs=OUT_BUFS))
         psum = ctx.enter_context(tc.psum_pool(name="psum", bufs=1))
         ctx.enter_context(tc.manual_schedule())
 
         def bank(index, shape, dtype=F32):
             return psum.tile(shape, dtype, name="bank%d" % index, tag="bank%d" % index)
 
-        xs = [keep.tile([P, TILES // 2, D], BF16, name="xs%d" % h, align_bytes=64) for h in range(2)]
-        w1w = [keep.tile([P, F2], U8, name="w1w%d" % h, align_bytes=64) for h in range(2)]
+        xs = keep.tile([P, TILES, D], BF16, align_bytes=64)
+        w1_first = keep.tile([P, 2, W1_BYTES], U8, align_bytes=64)
+        w1_rest = keep.tile([P, 2, F2 - W1_BYTES], U8, align_bytes=64)
         w1s = keep.tile([P, F2], U8, align_bytes=64)
         w2w = keep.tile([P, 2, 2 * D], U8, align_bytes=64)
         w2s = keep.tile([P, 2, D], U8, align_bytes=64)
@@ -62,323 +80,374 @@ def tile_sanamixffndepthwiseglu_x2_kernel(
         ident = keep.tile([P, P], F32, align_bytes=64)
         ident_bf = keep.tile([P, P], BF16, align_bytes=64)
         perm = keep.tile([P, P], F32, align_bytes=64)
-        zeros = keep.tile([P, LEAD + PITCH], F32, align_bytes=64)
-        u = [keep.tile([P, U_LEN], F32, name="u%d" % i, align_bytes=64) for i in range(U_BUFS)]
-        xg = keep.tile([P, TOK, 4], BF16, align_bytes=64)
-        xc = keep.tile([P, TOK], U32, align_bytes=64)
-        xsc = keep.tile([P, TOK], U8, align_bytes=64)
-        gt = keep.tile([P, TILES, 2, 2, 2 * P], BF16, align_bytes=64)
-        gg = keep.tile([P, 2, TOK, 4], BF16, align_bytes=64)
-        gc = keep.tile([P, 2, TOK], U32, align_bytes=64)
-        gsc = keep.tile([P, 2, TOK], U8, align_bytes=64)
-        og = keep.tile([P, TOK, 4], BF16, align_bytes=64)
-        oc = keep.tile([P, TOK], U32, align_bytes=64)
-        osc = keep.tile([P, TOK], U8, align_bytes=64)
+        zeros = keep.tile([P, GRID], F32, align_bytes=64)
+        u = keep.tile([P, U_BUFS, U_LEN], F32, name="u", align_bytes=64)
+        top = keep.tile([P, TOP_BUFS, TOK], F32, name="top", align_bytes=64)
+        x_woven = keep.tile([P, TOK, 4], BF16, align_bytes=64)
+        x_codes = keep.tile([P, TOK], U32, align_bytes=64)
+        x_scales = keep.tile([P, TOK], U8, align_bytes=64)
+        g_tok = keep.tile([P, TILES, 2, 2, 2 * P], BF16, align_bytes=64)
+        g_woven = keep.tile([P, 2, TOK, 4], BF16, align_bytes=64)
+        g_codes = keep.tile([P, 2, TOK], U32, align_bytes=64)
+        g_scales = keep.tile([P, 2, TOK], U8, align_bytes=64)
+        o_woven = keep.tile([P, TOK, 4], BF16, align_bytes=64)
+        o_codes = keep.tile([P, TOK], U32, align_bytes=64)
+        o_scales = keep.tile([P, TOK], U8, align_bytes=64)
 
-        nc.scalar.dma_start(out=xs[0][:], in_=x_rows[:, 0:4, :])
+        nc.sync.dma_start(out=xs[:, 0:2, :], in_=x_tiles[:, 0:2, :])
+        nc.vector.memset(rows_b[:], 0.0)
         nc.vector.memset(zeros[:], 0.0)
         nc.vector.memset(w1s[:].bitcast(U32), 0)
-        nc.vector.memset(rows_b[:], 0.0)
-        nc.scalar.activation(out=u[0][:, 0 : LEAD + PITCH], in_=zeros[:], func=ACT.Silu)
+        nc.scalar.activation(out=top[:, 0, 0:GRID], in_=zeros[:], func=ACT.Silu)
         make_identity(nc, ident[:])
-        nc.sync.dma_start(out=xs[1][:], in_=x_rows[:, 4:8, :])
-        nc.sync.dma_start(out=w1w[1][:].bitcast(I32), in_=w1_words[0, :, F2 : 2 * F2].bitcast(I32))
-        nc.sync.dma_start(out=rows_b[16:32, :], in_=b1.rearrange("(m c) -> m c", c=P))
-        nc.sync.dma_start(out=rows_b[0:16, :], in_=wd_rows[P : P + 16, :])
-        nc.sync.dma_start(out=rows_b[32:40, :], in_=gain.rearrange("(m c) -> m c", c=P))
-        for quad in range(4):
+        last_tap = TAPS * CHUNKS - P
+        nc.sync.dma_start(out=rows_b[BIAS_COL - P : GAIN_COL - P, :], in_=b1.rearrange("(m c) -> m c", c=P))
+        nc.sync.dma_start(out=rows_b[0:last_tap, :], in_=wd_rows[P : P + last_tap, :])
+        nc.sync.dma_start(out=rows_b[GAIN_COL - P : GAIN_COL - P + PAIRS, :], in_=gain.rearrange("(m c) -> m c", c=P))
+        nc.sync.dma_start(out=rows_a[:], in_=wd_rows[0:P, :])
+        nc.sync.dma_start(out=xs[:, 2:4, :], in_=x_tiles[:, 2:4, :])
+        nc.sync.dma_start(out=xs[:, 4:TILES, :], in_=x_tiles[:, 4:TILES, :])
+        nc.sync.dma_start(out=w1_first[:].bitcast(I32), in_=w1_branches[:, :, 0:W1_BYTES].bitcast(I32))
+        for quad in range(QUADS):
             nc.sync.dma_start(
                 out=w1s[32 * quad : 32 * quad + 4, :].bitcast(I32),
                 in_=w1_scales[0, 4 * quad : 4 * quad + 4, :].bitcast(I32),
             )
-        nc.sync.dma_start(out=rows_a[:], in_=wd_rows[0:P, :])
-        nc.sync.dma_start(out=w1w[0][:].bitcast(I32), in_=w1_words[0, :, 0:F2].bitcast(I32))
+        nc.sync.dma_start(out=w1_rest[:].bitcast(I32), in_=w1_branches[:, :, W1_BYTES:].bitcast(I32))
 
         nc.vector.tensor_copy(out=ident_bf[:], in_=ident[:])
         nc.vector.tensor_copy(
             out=perm[:].rearrange("p (u c e) -> p u c e", u=2, e=2),
             in_=ident[:].rearrange("p (c u e) -> p u c e", u=2, e=2),
         )
-        nc.vector.memset(u[0][:, LEAD + PITCH :], 0.0)
-        for i in range(1, U_BUFS):
-            nc.vector.memset(u[i][:], 0.0)
+        nc.vector.memset(u[:].rearrange("p b (i j) -> p b i j", j=PITCH)[:, :, :, 0:LEAD], 0.0)
+        nc.vector.memset(u[:, :, PITCH * GRID + LEAD : PITCH * (GRID + 1)], 0.0)
+        nc.vector.memset(top[:, 1:, 0:GRID], 0.0)
         nc.vector.memset(w2s[:].rearrange("p g n -> p (g n)").bitcast(U32), 0)
         nc.sync.dma_start(out=w2w[:].bitcast(I32), in_=w2_words.rearrange("g p n -> p g n").bitcast(I32))
-        for quad in range(4):
+        for quad in range(QUADS):
             nc.sync.dma_start(
                 out=w2s[32 * quad : 32 * quad + 4, :, :].bitcast(I32),
                 in_=w2_scales[:, 4 * quad : 4 * quad + 4, :].rearrange("g r n -> r g n").bitcast(I32),
             )
 
-        def turn_words(index, sources):
-            pt = bank(index, [P, 2, 2, P])
-            for qq in range(2):
-                for half in range(2):
-                    nc.tensor.transpose(pt[:, qq, half, :], sources[qq][half], ident[:])
-            return pt
-
-        def weave(engine, grouped, pt):
-            dst = grouped.bitcast(F32).rearrange("p (q r) u -> p q r u", q=2)
-            src = pt[:].rearrange("p q u r -> p q r u")
+        def copy(engine, dst, src):
             if engine == "scalar":
                 nc.scalar.copy(out=dst, in_=src)
             else:
                 nc.vector.tensor_copy(out=dst, in_=src)
 
-        def quantize(grouped, codes, scales):
-            nc.vector.quantize_mx(out=codes.bitcast(FP8X4), scales=scales, in_=grouped.rearrange("p r t -> p (r t)"))
+        def turn(index, words):
+            turned = bank(index, [P, len(words), 2, P])
+            for q in range(len(words)):
+                for half in range(2):
+                    nc.tensor.transpose(turned[:, q, half, :], words[q][half], ident[:])
+            return turned
 
-        def x_sources(r):
-            res = []
-            for qq in range(2):
-                q = 2 * r + qq
-                words = xs[q // 4][:, q % 4, :].bitcast(F32)
-                res.append([words[:, half : 2 * P : 2] for half in range(2)])
-            return res
+        def weave(engine, woven, turned):
+            copy(
+                engine,
+                woven.bitcast(F32).rearrange("p (q m) u -> p q m u", m=P),
+                turned[:].rearrange("p q u m -> p q m u"),
+            )
 
-        order = [c for j in range(PAIRS) for c in (PAIRS + j, j)]
-        hbank = {}
+        def quantize(woven, codes, scales):
+            nc.vector.quantize_mx(out=codes.bitcast(FP8X4), scales=scales, in_=woven.rearrange("p m t -> p (m t)"))
 
-        def expand(s, h):
-            c = order[s]
-            hb = bank(2 * (s % 2) + h, [P, BANK])
-            hbank[s, h] = hb
-            w = w1w[c // PAIRS]
-            off = 2 * P * (c % PAIRS)
+        def x_turn(q0, index):
+            words = [xs[:, q, :].bitcast(F32) for q in (q0, q0 + 1)]
+            return turn(index, [[w[:, half : 2 * P : 2] for half in range(2)] for w in words])
+
+        def x_quant(m0, m1):
+            quantize(x_woven[:, m0:m1, :], x_codes[:, m0:m1], x_scales[:, m0:m1])
+
+        chunk_of = [c for j in range(PAIRS) for c in (PAIRS + j, j)]
+        h_banks = {}
+
+        def expand(slot, half):
+            chunk = chunk_of[slot]
+            branch, j = divmod(chunk, PAIRS)
+            words = w1_first[:, branch, :] if j == 0 else w1_rest[:, branch, W1_BYTES * (j - 1) : W1_BYTES * j]
+            tokens = slice(HALF * half, HALF * (half + 1))
+            h_banks[slot, half] = bank(2 * (slot % 2) + half, [P, HALF])
             nc.tensor.matmul_mx(
-                out=hb[:],
-                lhsT=w[:, off : off + 2 * P].bitcast(FP4X4),
-                lhsT_scale=w1s[:, P * c : P * (c + 1)],
-                rhs=xc[:, BANK * h : BANK * (h + 1)].bitcast(FP8X4),
-                rhs_scale=xsc[:, BANK * h : BANK * (h + 1)],
+                out=h_banks[slot, half][:],
+                lhsT=words.bitcast(FP4X4),
+                lhsT_scale=w1s[:, P * chunk : P * (chunk + 1)],
+                rhs=x_codes[:, tokens].bitcast(FP8X4),
+                rhs_scale=x_scales[:, tokens],
                 start=True,
                 stop=True,
             )
 
-        def window(s, r, t):
-            first = LEAD + PITCH * r + t - 1
-            return u[s % U_BUFS][:, first : first + PITCH * GRID].rearrange("p (i j) -> p i j", j=PITCH)[:, :, 0:GRID]
+        def window(slot, tap, i0, i1):
+            first = LEAD + PITCH * (i0 + tap // 3 - 1) + tap % 3 - 1
+            rows = u[:, slot % U_BUFS, first : first + PITCH * (i1 - i0)]
+            return rows.rearrange("p (i j) -> p i j", j=PITCH)[:, :, 0:GRID]
 
-        def activate(s, h):
-            c = order[s]
-            half_rows = GRID // 2
+        def activate(slot, half):
+            col = BIAS_COL + chunk_of[slot]
             nc.scalar.activation(
-                out=window(s, 1, 1)[:, half_rows * h : half_rows * (h + 1), :],
-                in_=hbank[s, h][:].rearrange("p (i j) -> p i j", j=GRID),
+                out=window(slot, 4, GRID // 2 * half, GRID // 2 * (half + 1)),
+                in_=h_banks[slot, half][:].rearrange("p (i j) -> p i j", j=GRID),
                 func=ACT.Silu,
-                bias=cols[:, 9 * CHUNKS + c : 9 * CHUNKS + c + 1],
+                bias=cols[:, col : col + 1],
             )
 
-        def weight(s, tap):
-            col = CHUNKS * tap + order[s]
+        def weight(slot, tap):
+            col = CHUNKS * tap + chunk_of[slot]
             return cols[:, col : col + 1]
 
-        def product(engine, s, tap):
-            pr = prods.tile([P, TOK], F32, name="pr", tag="pr")
-            dst = pr[:].rearrange("p (i j) -> p i j", j=GRID)
-            src = window(s, tap // 3, tap % 3)
-            if engine == "scalar":
-                nc.scalar.activation(out=dst, in_=src, func=ACT.Copy, scale=weight(s, tap))
-            else:
-                nc.vector.tensor_scalar(out=dst, in0=src, scalar1=weight(s, tap), scalar2=None, op0=ALU.mult)
-            return pr
+        def grid_rows(tile, i0, i1):
+            return tile[:, GRID * i0 : GRID * i1].rearrange("p (i j) -> p i j", j=GRID)
 
-        def add_product(s, tap, pr):
-            dst = pr[:].rearrange("p (i j) -> p i j", j=GRID)
+        tops_made = []
+
+        def top_product(unit, tap):
+            slot, q0, q1 = unit
+            tile = top[:, len(tops_made) % TOP_BUFS, :]
+            tops_made.append(tap)
+            i0, i1 = max(1, ROWS * q0), ROWS * q1
+            nc.scalar.activation(
+                out=grid_rows(tile, i0, i1), in_=window(slot, tap, i0, i1), func=ACT.Copy, scale=weight(slot, tap)
+            )
+            return tile
+
+        def product(engine, unit, tap):
+            slot, q0, q1 = unit
+            tile = prods.tile([P, TOK], F32, name="pr", tag="pr")
+            dst, src = grid_rows(tile, ROWS * q0, ROWS * q1), window(slot, tap, ROWS * q0, ROWS * q1)
+            if engine == "scalar":
+                nc.scalar.activation(out=dst, in_=src, func=ACT.Copy, scale=weight(slot, tap))
+            else:
+                nc.vector.tensor_scalar(out=dst, in0=src, scalar1=weight(slot, tap), scalar2=None, op0=ALU.mult)
+            return tile
+
+        def add_product(unit, tap, tile):
+            slot, q0, q1 = unit
+            i0, i1 = ROWS * q0, min(GRID - 1, ROWS * q1)
+            dst = grid_rows(tile, i0, i1)
             nc.vector.scalar_tensor_tensor(
-                out=dst, in0=window(s, tap // 3, tap % 3), scalar=weight(s, tap), in1=dst, op0=ALU.mult, op1=ALU.add
+                out=dst, in0=window(slot, tap, i0, i1), scalar=weight(slot, tap), in1=dst, op0=ALU.mult, op1=ALU.add
             )
 
-        cbank = {}
+        def spans(unit):
+            slot, q0, q1 = unit
+            return [(slot, q, min(q + BANK_TILES, q1)) for q in range(q0, q1, BANK_TILES)]
 
-        def accumulate(s, pr, first, last):
-            for h in range(2):
+        c_banks = {}
+
+        def accumulate(unit, tile, first, last):
+            for span in spans(unit):
+                slot, q0, q1 = span
                 if first:
-                    cbank[s, h] = bank(4 + 2 * (s % 2) + h, [P, 4, P])
-                for qq in range(4):
-                    q = 4 * h + qq
+                    c_banks[span] = bank(SUM_BANK + len(c_banks) % 4, [P, q1 - q0, P])
+                for q in range(q0, q1):
                     nc.tensor.matmul(
-                        out=cbank[s, h][:, qq, :],
-                        lhsT=pr[:, P * q : P * (q + 1)],
+                        out=c_banks[span][:, q - q0, :],
+                        lhsT=tile[:, P * q : P * (q + 1)],
                         rhs=perm[:],
                         is_transpose=True,
-                        start=(first and qq == 0),
-                        stop=(last and qq == 3),
+                        start=(first and q == q0),
+                        stop=(last and q == q1 - 1),
                     )
 
-        gate = {}
+        silu_cb = {}
 
-        def gate_silu(s, h):
-            gate[h] = gates.tile([P, 4, P], F32, name="gate", tag="gate")
-            nc.scalar.activation(out=gate[h][:], in_=cbank[s, h][:], func=ACT.Silu)
+        def drain(unit):
+            for span in spans(unit):
+                slot, q0, q1 = span
+                if slot % 2 == 0:
+                    gate = gates.tile([P, q1 - q0, P], F32, name="gate", tag="gate")
+                    nc.scalar.activation(out=gate[:], in_=c_banks[span][:], func=ACT.Silu)
+                    for q in range(q0, q1):
+                        silu_cb[q] = (gate, q0)
+                else:
+                    group, j = divmod(chunk_of[slot], 4)
+                    gate, base = silu_cb[q0]
+                    nc.vector.tensor_tensor(
+                        out=g_tok[:, q0:q1, group, :, P // 2 * j : P // 2 * (j + 1)],
+                        in0=c_banks[span][:].rearrange("p q (u c) -> p q u c", u=2),
+                        in1=gate[:, q0 - base : q1 - base, :].rearrange("p q (u c) -> p q u c", u=2),
+                        op=ALU.mult,
+                    )
 
-        def gate_mul(s, h):
-            j = order[s]
-            nc.vector.tensor_tensor(
-                out=gt[:, 4 * h : 4 * h + 4, j // 4, :, 64 * (j % 4) : 64 * (j % 4 + 1)],
-                in0=cbank[s, h][:].rearrange("p q (u c) -> p q u c", u=2),
-                in1=gate[h][:].rearrange("p q (u c) -> p q u c", u=2),
-                op=ALU.mult,
-            )
+        g_turned, o_turned, o_banks, o32, o16 = {}, {}, {}, {}, {}
 
-        def g_sources(group, r):
-            return [[gt[:, 2 * r + qq, group, half, :].bitcast(F32) for half in range(2)] for qq in range(2)]
+        def g_turn(group, q0, index):
+            words = [[g_tok[:, q, group, half, :].bitcast(F32) for half in range(2)] for q in (q0, q0 + 1)]
+            g_turned[q0] = turn(index, words)
 
-        xt = [turn_words(4 + r, x_sources(r)) for r in range(2)]
-        ct = bank(3, [P, 2, P], BF16)
-        nc.tensor.transpose(ct[:, 1, :], rows_b[:], ident_bf[:])
-        nc.tensor.transpose(ct[:, 0, :], rows_a[:], ident_bf[:])
-        xt += [turn_words(4 + r, x_sources(r)) for r in range(2, 4)]
-        weave("vector", xg[:, 0:256, :], xt[0])
-        weave("scalar", xg[:, 256:512, :], xt[1])
-        nc.vector.tensor_copy(out=cols[:], in_=ct[:].rearrange("p a c -> p (a c)"))
-        quantize(xg[:, 0:512, :], xc[:, 0:512], xsc[:, 0:512])
-        weave("scalar", xg[:, 768:1024, :], xt[3])
-        weave("vector", xg[:, 512:768, :], xt[2])
-        taps = cols[:, 0 : 9 * CHUNKS].rearrange("p (k m) -> p k m", m=CHUNKS)[:, :, 0:PAIRS]
-        nc.vector.tensor_tensor(
-            out=taps,
-            in0=taps,
-            in1=cols[:, 10 * CHUNKS : 10 * CHUNKS + PAIRS].unsqueeze(1).to_broadcast([P, 9, PAIRS]),
-            op=ALU.mult,
-        )
-        quantize(xg[:, 512:1024, :], xc[:, 512:1024], xsc[:, 512:1024])
-        expand(0, 0)
-        expand(1, 0)
-        expand(0, 1)
-        expand(1, 1)
-        activate(0, 0)
-        activate(0, 1)
+        def g_weave(group, q0):
+            weave("scalar", g_woven[:, group, P * q0 : P * (q0 + 2), :], g_turned[q0])
 
-        gpt = {}
-        for s in range(CHUNKS):
-            p1 = product("scalar", s, 0)
-            pa = product("vector", s, 1)
-            pc = product("vector", s, 4)
-            accumulate(s, pc, True, False)
-            accumulate(s, p1, False, False)
-            if s + 1 < CHUNKS:
-                activate(s + 1, 0)
-                activate(s + 1, 1)
-            if s in (10, 12):
-                for k in range(2):
-                    r = s - 10 + k
-                    weave("scalar", gg[:, 0, 256 * r : 256 * (r + 1), :], gpt[r])
-            pb = product("vector", s, 7)
-            pd = product("vector", s, 3)
-            p2 = product("scalar", s, 2)
-            accumulate(s, pd, False, False)
-            accumulate(s, p2, False, False)
-            if s % 2 == 1:
-                gate_silu(s - 1, 0)
-                gate_silu(s - 1, 1)
-            elif s > 0:
-                gate_mul(s - 1, 0)
-                gate_mul(s - 1, 1)
-            if s in (11, 13):
-                lo = 512 * ((s - 11) // 2)
-                quantize(gg[:, 0, lo : lo + 512, :], gc[:, 0, lo : lo + 512], gsc[:, 0, lo : lo + 512])
-            add_product(s, 5, pa)
-            p3 = product("scalar", s, 6)
-            accumulate(s, pa, False, False)
-            add_product(s, 8, pb)
-            accumulate(s, p3, False, False)
-            accumulate(s, pb, False, True)
-            if s % 2 == 0 and s + 2 < CHUNKS:
-                for k in (2, 3):
-                    expand(s + k, 0)
-                    expand(s + k, 1)
-            if s in (9, 11):
-                for k in range(2):
-                    r = s - 9 + k
-                    gpt[r] = turn_words(k, g_sources(0, r))
+        def g_quant(group, q0, q1):
+            tokens = slice(P * q0, P * q1)
+            quantize(g_woven[:, group, tokens, :], g_codes[:, group, tokens], g_scales[:, group, tokens])
 
-        last = CHUNKS - 1
-        o32 = {}
-        ob = {}
-        acc = {}
-        opt = {}
-
-        def g_turn(r):
-            gpt[r] = turn_words((4, 5, 6, 7)[r], g_sources(1, r))
-
-        def g_weave(r):
-            weave("scalar", gg[:, 1, 256 * r : 256 * (r + 1), :], gpt[r])
-
-        def g_quant(r):
-            cs = slice(256 * r, 256 * (r + 1))
-            quantize(gg[:, 1, cs, :], gc[:, 1, cs], gsc[:, 1, cs])
-
-        def project(q):
-            acc[q] = bank(q % 4, [P, D])
+        def project(q, index):
+            o_banks[q] = bank(index, [P, D])
             for group in range(2):
                 nc.tensor.matmul_mx(
-                    out=acc[q][:],
-                    lhsT=gc[:, group, P * q : P * (q + 1)].bitcast(FP8X4),
-                    lhsT_scale=gsc[:, group, P * q : P * (q + 1)],
+                    out=o_banks[q][:],
+                    lhsT=g_codes[:, group, P * q : P * (q + 1)].bitcast(FP8X4),
+                    lhsT_scale=g_scales[:, group, P * q : P * (q + 1)],
                     rhs=w2w[:, group, :].bitcast(FP4X4),
                     rhs_scale=w2s[:, group, :],
                     start=(group == 0),
                     stop=(group == 1),
                 )
 
-        def evacuate(q):
+        def evacuate(q, engine="scalar"):
             o32[q] = outs.tile([P, D], F32, name="o32", tag="o32")
-            nc.scalar.copy(out=o32[q][:], in_=acc[q][:])
+            copy(engine, o32[q][:], o_banks[q][:])
             nc.sync.dma_start(out=out_rows[P * q : P * (q + 1), :], in_=o32[q][:])
 
         def narrow(q):
-            ob[q] = outs.tile([P, 2, 2 * P], BF16, name="ob", tag="ob")
+            o16[q] = outs.tile([P, 2, 2 * P], BF16, name="o16", tag="o16")
             nc.vector.tensor_copy(
-                out=ob[q][:].rearrange("p u (c e) -> p u c e", e=2),
+                out=o16[q][:].rearrange("p u (c e) -> p u c e", e=2),
                 in_=o32[q][:].rearrange("p (c u e) -> p u c e", u=2, e=2),
             )
 
-        def o_turn(r):
-            opt[r] = turn_words(4 + r, [[ob[2 * r + qq][:, half, :].bitcast(F32) for half in range(2)] for qq in range(2)])
+        def o_turn(q0, index):
+            o_turned[q0] = turn(index, [[o16[q][:, half, :].bitcast(F32) for half in range(2)] for q in (q0, q0 + 1)])
 
-        def o_weave(r):
-            weave("vector", og[:, 256 * r : 256 * (r + 1), :], opt[r])
+        def o_weave(q0, engine):
+            weave(engine, o_woven[:, P * q0 : P * (q0 + 2), :], o_turned[q0])
 
-        def o_quant(r):
-            cs = slice(256 * r, 256 * (r + 1))
-            quantize(og[:, cs, :], oc[:, cs], osc[:, cs])
-            nc.sync.dma_start(out=out_words[:, cs], in_=oc[:, cs].bitcast(I32))
+        def o_quant(half):
+            tokens = slice(HALF * half, HALF * (half + 1))
+            quantize(o_woven[:, tokens, :], o_codes[:, tokens], o_scales[:, tokens])
+            nc.sync.dma_start(out=out_words[:, tokens], in_=o_codes[:, tokens].bitcast(I32))
 
-        gate_mul(last, 0)
-        g_turn(0)
-        g_turn(1)
-        gate_mul(last, 1)
-        g_weave(0)
-        g_weave(1)
-        g_turn(2)
-        g_turn(3)
-        g_quant(0)
-        g_quant(1)
+        x_turned = [x_turn(0, SUM_BANK)]
+        cols_bank = bank(3, [P, 2, P], BF16)
+        nc.tensor.transpose(cols_bank[:, 1, :], rows_b[:], ident_bf[:])
+        nc.tensor.transpose(cols_bank[:, 0, :], rows_a[:], ident_bf[:])
+        x_turned += [x_turn(2 * r, SUM_BANK + r) for r in range(1, 4)]
+        weave("vector", x_woven[:, 0 : 2 * P, :], x_turned[0])
+        weave("scalar", x_woven[:, 2 * P : HALF, :], x_turned[1])
+        nc.vector.tensor_copy(out=cols[:], in_=cols_bank[:].rearrange("p a c -> p (a c)"))
+        x_quant(0, 2 * P)
+        linear_taps = cols[:, 0:BIAS_COL].rearrange("p (k m) -> p k m", m=CHUNKS)[:, :, 0:PAIRS]
+        nc.vector.tensor_tensor(
+            out=linear_taps,
+            in0=linear_taps,
+            in1=cols[:, GAIN_COL : GAIN_COL + PAIRS].unsqueeze(1).to_broadcast([P, TAPS, PAIRS]),
+            op=ALU.mult,
+        )
+        x_quant(2 * P, HALF)
+        expand(0, 0)
+        expand(1, 0)
+        weave("scalar", x_woven[:, HALF : HALF + 2 * P, :], x_turned[2])
+        weave("vector", x_woven[:, HALF + 2 * P : TOK, :], x_turned[3])
+        activate(0, 0)
+        x_quant(HALF, TOK)
+
+        units = [(0, 0, 3), (1, 0, 3), (0, 3, TILES), (1, 3, TILES)]
+        units += [(slot, 0, TILES) for slot in range(2, CHUNKS - 4)]
+        units += [(slot, 0, 4) for slot in range(CHUNKS - 4, CHUNKS)]
+        second = len(units)
+        units += [(slot, 4, TILES) for slot in range(CHUNKS - 4, CHUNKS - 1)]
+        units += [(CHUNKS - 1, 4, 6), (CHUNKS - 1, 6, TILES)]
+
+        placed = {}
+
+        def place(n, mark, step, *args):
+            placed.setdefault((n, mark), []).append((step, args))
+
+        def run(n, mark):
+            for step, args in placed.get((n, mark), []):
+                step(*args)
+
+        place(0, "s_early", activate, 1, 0)
+        place(0, "t_early", expand, 0, 1)
+        place(0, "t_early", expand, 1, 1)
+        place(0, "s_late", activate, 0, 1)
+        place(1, "s_early", activate, 1, 1)
+        for slot in range(2, CHUNKS):
+            for half in range(2):
+                place(slot - slot % 2 - 1, "t_late", expand, slot, half)
+                place(slot, "s_late", activate, slot, half)
+        for half in range(2):
+            n = 11 + 2 * half
+            for k in range(2):
+                place(n, "t_early", g_turn, 0, 4 * half + 2 * k, k)
+                place(n, "s_late", g_weave, 0, 4 * half + 2 * k)
+            place(n + 1, "v_late", g_quant, 0, 4 * half, 4 * half + 4)
+        for k in range(2):
+            place(second, "t_late", g_turn, 1, 2 * k, k)
+            place(second + 1, "s_late", g_weave, 1, 2 * k)
+        place(second + 2, "v_mid", g_quant, 1, 0, 4)
         for q in range(4):
-            project(q)
-        g_weave(2)
-        g_weave(3)
-        g_quant(2)
-        g_quant(3)
-        for r in range(4):
-            evacuate(2 * r)
-            evacuate(2 * r + 1)
-            if r < 2:
-                project(2 * r + 4)
-                project(2 * r + 5)
-            narrow(2 * r)
-            narrow(2 * r + 1)
-            if r > 0:
-                o_weave(r - 1)
-            if r > 1:
-                o_quant(r - 2)
-            o_turn(r)
-        o_quant(2)
-        o_weave(3)
-        o_quant(3)
-        for quad in range(4):
+            place(second + 2, "t_early", project, q, (q + 2) % 4)
+        for q in range(2):
+            place(second + 2, "s_late", evacuate, q)
+            place(second + 3, "v_late", narrow, q)
+            place(second + 4, "s_late", evacuate, q + 2)
+        place(second + 3, "t_late", o_turn, 0, 2)
+        place(second + 4, "t_late", g_turn, 1, 4, 3)
+
+        for n, unit in enumerate(units):
+            slot, q0, q1 = unit
+            n_added = 3 if (slot % 2 == 1 and q1 - q0 == TILES) or n >= second else 2
+            scalar_takes_5 = n >= len(units) - 3
+            vector_taps = ([3, 4] if scalar_takes_5 else [3, 4, 5]) + list(range(6, TAPS - n_added))
+
+            top0 = top_product(unit, 0)
+            made = [product("vector", unit, tap) for tap in vector_taps]
+            run(n, "s_early")
+            run(n, "v_mid")
+            top1 = top_product(unit, 1)
+            top2 = top_product(unit, 2)
+            fifth = [product("scalar", unit, 5)] if scalar_takes_5 else []
+            for k in range(n_added):
+                add_product(unit, TAPS - n_added + k, made[k % len(made)])
+            if n > 0:
+                drain(units[n - 1])
+            run(n, "v_late")
+            plain = made[n_added:]
+            added = [made[k % len(made)] for k in range(n_added)][-len(made) :]
+            tiles = plain[:1] + [top0] + plain[1:] + [top1] + added[:1] + [top2] + added[1:] + fifth
+            for k, tile in enumerate(tiles):
+                if k == 2:
+                    run(n, "t_early")
+                accumulate(unit, tile, k == 0, k == len(tiles) - 1)
+            run(n, "s_late")
+            run(n, "t_late")
+
+        drain(units[-1])
+        g_weave(1, 4)
+        g_turn(1, 6, 7)
+        narrow(2)
+        narrow(3)
+        g_quant(1, 4, 6)
+        g_weave(1, 6)
+        project(4, 4)
+        project(5, 5)
+        o_turn(2, 0)
+        o_weave(0, "vector")
+        g_quant(1, 6, TILES)
+        project(6, 6)
+        project(7, 1)
+        evacuate(4)
+        evacuate(5, "vector")
+        o_weave(2, "scalar")
+        narrow(4)
+        narrow(5)
+        o_turn(4, 3)
+        evacuate(6)
+        evacuate(7)
+        o_quant(0)
+        narrow(6)
+        narrow(7)
+        o_turn(6, 7)
+        o_weave(4, "vector")
+        o_weave(6, "scalar")
+        o_quant(1)
+        for quad in range(QUADS):
             nc.sync.dma_start(
                 out=out_2[0, 4 * quad : 4 * quad + 4, :].bitcast(I32),
-                in_=osc[32 * quad : 32 * quad + 4, :].bitcast(I32),
+                in_=o_scales[32 * quad : 32 * quad + 4, :].bitcast(I32),
             )

@@ -39,6 +39,8 @@ PROD_BUFS = 9
 GATE_BUFS = 4
 OUT_BUFS = 4
 
+WARM_UP = 10
+
 BIAS_COL = TAPS * CHUNKS
 GAIN_COL = BIAS_COL + CHUNKS
 
@@ -100,6 +102,9 @@ def tile_sanamixffndepthwiseglu_x2_kernel(
         nc.vector.memset(w1s[:].bitcast(U32), 0)
         nc.scalar.activation(out=top[:, 0, 0:GRID], in_=zeros[:], func=ACT.Silu)
         make_identity(nc, ident[:])
+        warm = bank(0, [P, BANK_TILES, P])
+        for k in range(WARM_UP):
+            nc.tensor.transpose(warm[:, k % BANK_TILES, :], ident[:], ident[:])
         last_tap = TAPS * CHUNKS - P
         nc.sync.dma_start(out=rows_b[BIAS_COL - P : GAIN_COL - P, :], in_=b1.rearrange("(m c) -> m c", c=P))
         nc.sync.dma_start(out=rows_b[0:last_tap, :], in_=wd_rows[P : P + last_tap, :])
@@ -274,12 +279,12 @@ def tile_sanamixffndepthwiseglu_x2_kernel(
 
         g_turned, o_turned, o_banks, o32, o16 = {}, {}, {}, {}, {}
 
-        def g_turn(group, q0, index):
-            words = [[g_tok[:, q, group, half, :].bitcast(F32) for half in range(2)] for q in (q0, q0 + 1)]
+        def g_turn(group, q0, index, n=2):
+            words = [[g_tok[:, q, group, half, :].bitcast(F32) for half in range(2)] for q in range(q0, q0 + n)]
             g_turned[q0] = turn(index, words)
 
-        def g_weave(group, q0):
-            weave("scalar", g_woven[:, group, P * q0 : P * (q0 + 2), :], g_turned[q0])
+        def g_weave(group, q0, n=2):
+            weave("scalar", g_woven[:, group, P * q0 : P * (q0 + n), :], g_turned[q0])
 
         def g_quant(group, q0, q1):
             tokens = slice(P * q0, P * q1)
@@ -303,21 +308,22 @@ def tile_sanamixffndepthwiseglu_x2_kernel(
             copy(engine, o32[q][:], o_banks[q][:])
             nc.sync.dma_start(out=out_rows[P * q : P * (q + 1), :], in_=o32[q][:])
 
-        def narrow(q):
+        def narrow(q, engine="vector", source=o32):
             o16[q] = outs.tile([P, 2, 2 * P], BF16, name="o16", tag="o16")
-            nc.vector.tensor_copy(
-                out=o16[q][:].rearrange("p u (c e) -> p u c e", e=2),
-                in_=o32[q][:].rearrange("p (c u e) -> p u c e", u=2, e=2),
+            copy(
+                engine,
+                o16[q][:].rearrange("p u (c e) -> p u c e", e=2),
+                source[q][:].rearrange("p (c u e) -> p u c e", u=2, e=2),
             )
 
-        def o_turn(q0, index):
-            o_turned[q0] = turn(index, [[o16[q][:, half, :].bitcast(F32) for half in range(2)] for q in (q0, q0 + 1)])
+        def o_turn(q0, index, n=2):
+            o_turned[q0] = turn(index, [[o16[q][:, half, :].bitcast(F32) for half in range(2)] for q in range(q0, q0 + n)])
 
-        def o_weave(q0, engine):
-            weave(engine, o_woven[:, P * q0 : P * (q0 + 2), :], o_turned[q0])
+        def o_weave(q0, engine, n=2):
+            weave(engine, o_woven[:, P * q0 : P * (q0 + n), :], o_turned[q0])
 
-        def o_quant(half):
-            tokens = slice(HALF * half, HALF * (half + 1))
+        def o_quant(q0, q1):
+            tokens = slice(P * q0, P * q1)
             quantize(o_woven[:, tokens, :], o_codes[:, tokens], o_scales[:, tokens])
             nc.sync.dma_start(out=out_words[:, tokens], in_=o_codes[:, tokens].bitcast(I32))
 
@@ -404,7 +410,9 @@ def tile_sanamixffndepthwiseglu_x2_kernel(
             fifth = [product("scalar", unit, 5)] if scalar_takes_5 else []
             for k in range(n_added):
                 add_product(unit, TAPS - n_added + k, made[k % len(made)])
-            if n > 0:
+            if n == len(units) - 1:
+                drain(units[n - 2])
+            if n > 0 and n != len(units) - 2:
                 drain(units[n - 1])
             run(n, "v_late")
             plain = made[n_added:]
@@ -418,36 +426,41 @@ def tile_sanamixffndepthwiseglu_x2_kernel(
             run(n, "t_late")
 
         drain(units[-1])
+        g_turn(1, 6, 6, 1)
         g_weave(1, 4)
-        g_turn(1, 6, 7)
-        narrow(2)
-        narrow(3)
+        g_weave(1, 6, 1)
+        g_turn(1, 7, 7, 1)
         g_quant(1, 4, 6)
-        g_weave(1, 6)
+        narrow(2)
+        g_weave(1, 7, 1)
         project(4, 4)
-        project(5, 5)
-        o_turn(2, 0)
-        o_weave(0, "vector")
         g_quant(1, 6, TILES)
-        project(6, 6)
-        project(7, 1)
         evacuate(4)
+        narrow(3)
+        o_weave(0, "vector")
+        project(5, 5)
+        project(6, 1)
         evacuate(5, "vector")
-        o_weave(2, "scalar")
         narrow(4)
-        narrow(5)
-        o_turn(4, 3)
         evacuate(6)
-        evacuate(7)
-        o_quant(0)
+        o_turn(2, 0)
+        narrow(5)
         narrow(6)
-        narrow(7)
-        o_turn(6, 7)
-        o_weave(4, "vector")
-        o_weave(6, "scalar")
-        o_quant(1)
+        o_weave(2, "scalar")
+        project(7, 6)
+        o_turn(4, 3)
+        o_turn(6, 4, 1)
+        o_quant(0, 4)
+        narrow(7, "scalar", o_banks)
+        evacuate(7)
+        o_turn(7, 7, 1)
+        o_weave(6, "vector", 1)
+        o_weave(7, "vector", 1)
+        o_quant(6, TILES)
+        o_weave(4, "scalar")
+        o_quant(4, 6)
         for quad in range(QUADS):
-            nc.sync.dma_start(
+            nc.scalar.dma_start(
                 out=out_2[0, 4 * quad : 4 * quad + 4, :].bitcast(I32),
                 in_=o_scales[32 * quad : 32 * quad + 4, :].bitcast(I32),
             )

from contextlib import ExitStack

import concourse.mybir as mybir
from concourse.masks import make_identity

F32 = mybir.dt.float32
BF16 = mybir.dt.bfloat16
I32 = mybir.dt.int32
U32 = mybir.dt.uint32
U8 = mybir.dt.uint8
FP8X4 = mybir.dt.float8_e4m3fn_x4
FP4X4 = mybir.dt.float4_e2m1fn_x4
ACT = mybir.ActivationFunctionType
ALU = mybir.AluOpType

P = 128
GRID = 32
TOK = GRID * GRID
D = 512
F = 1024
F2 = 2 * F
TAPS = 9
CHUNKS = F2 // P
PAIRS = F // P
TILES = TOK // P
ROWS = P // GRID
HALF = TOK // 2
BANK_TILES = 4
QUADS = 4
W1_BYTES = 2 * P

LEAD = 4
PITCH = GRID + LEAD
U_LEN = PITCH * (GRID + 2)

U_BUFS = 4
TOP_BUFS = 6
PROD_BUFS = 9
GATE_BUFS = 4
OUT_BUFS = 4

WARM_UP = 10

BIAS_COL = TAPS * CHUNKS
GAIN_COL = BIAS_COL + CHUNKS

SUM_BANK = 4

FLOPS = 2 * TOK * D * F2 + 2 * TOK * F * D + 2 * TAPS * TOK * F2


def tile_sanamixffndepthwiseglu_x2_kernel(
    tc, x, w1_words, w1_scales, b1, wd, gain, w2_words, w2_scales, out_0, out_1, out_2
):
    nc = tc.nc
    x_tiles = x.rearrange("b i j k -> (b i j) k").rearrange("(q p) k -> p q k", p=P)
    out_rows = out_0.rearrange("b i j d -> (b i j) d")
    out_words = out_1.rearrange("g p m t -> p (g m t)").bitcast(I32)
    wd_rows = wd.rearrange("r t (m c) -> (r t m) c", c=P)
    w1_branches = w1_words.rearrange("g p (a n) -> p (g a) n", a=2)

    with ExitStack() as ctx:
        keep = ctx.enter_context(tc.tile_pool(name="keep", bufs=1))
        prods = ctx.enter_context(tc.tile_pool(name="prods", bufs=PROD_BUFS))
        gates = ctx.enter_context(tc.tile_pool(name="gates", bufs=GATE_BUFS))
        outs = ctx.enter_context(tc.tile_pool(name="outs", bufs=OUT_BUFS))
        psum = ctx.enter_context(tc.psum_pool(name="psum", bufs=1))
        ctx.enter_context(tc.manual_schedule())

        def bank(index, shape, dtype=F32):
            return psum.tile(shape, dtype, name="bank%d" % index, tag="bank%d" % index)

        xs = keep.tile([P, TILES, D], BF16, align_bytes=64)
        w1_first = keep.tile([P, 2, W1_BYTES], U8, align_bytes=64)
        w1_rest = keep.tile([P, 2, F2 - W1_BYTES], U8, align_bytes=64)
        w1s = keep.tile([P, F2], U8, align_bytes=64)
        w2w = keep.tile([P, 2, 2 * D], U8, align_bytes=64)
        w2s = keep.tile([P, 2, D], U8, align_bytes=64)
        rows_a = keep.tile([P, P], BF16, align_bytes=64)
        rows_b = keep.tile([P, P], BF16, align_bytes=64)
        cols = keep.tile([P, 2 * P], F32, align_bytes=64)
        ident = keep.tile([P, P], F32, align_bytes=64)
        ident_bf = keep.tile([P, P], BF16, align_bytes=64)
        perm = keep.tile([P, P], F32, align_bytes=64)
        zeros = keep.tile([P, GRID], F32, align_bytes=64)
        u = keep.tile([P, U_BUFS, U_LEN], F32, name="u", align_bytes=64)
        top = keep.tile([P, TOP_BUFS, TOK], F32, name="top", align_bytes=64)
        x_woven = keep.tile([P, TOK, 4], BF16, align_bytes=64)
        x_codes = keep.tile([P, TOK], U32, align_bytes=64)
        x_scales = keep.tile([P, TOK], U8, align_bytes=64)
        g_tok = keep.tile([P, TILES, 2, 2, 2 * P], BF16, align_bytes=64)
        g_woven = keep.tile([P, 2, TOK, 4], BF16, align_bytes=64)
        g_codes = keep.tile([P, 2, TOK], U32, align_bytes=64)
        g_scales = keep.tile([P, 2, TOK], U8, align_bytes=64)
        o_woven = keep.tile([P, TOK, 4], BF16, align_bytes=64)
        o_codes = keep.tile([P, TOK], U32, align_bytes=64)
        o_scales = keep.tile([P, TOK], U8, align_bytes=64)

        nc.sync.dma_start(out=xs[:, 0:2, :], in_=x_tiles[:, 0:2, :])
        nc.vector.memset(rows_b[:], 0.0)
        nc.vector.memset(zeros[:], 0.0)
        nc.vector.memset(w1s[:].bitcast(U32), 0)
        nc.scalar.activation(out=top[:, 0, 0:GRID], in_=zeros[:], func=ACT.Silu)
        make_identity(nc, ident[:])
        warm = bank(0, [P, BANK_TILES, P])
        for k in range(WARM_UP):
            nc.tensor.transpose(warm[:, k % BANK_TILES, :], ident[:], ident[:])
        last_tap = TAPS * CHUNKS - P
        nc.sync.dma_start(out=rows_b[BIAS_COL - P : GAIN_COL - P, :], in_=b1.rearrange("(m c) -> m c", c=P))
        nc.sync.dma_start(out=rows_b[0:last_tap, :], in_=wd_rows[P : P + last_tap, :])
        nc.sync.dma_start(out=rows_b[GAIN_COL - P : GAIN_COL - P + PAIRS, :], in_=gain.rearrange("(m c) -> m c", c=P))
        nc.sync.dma_start(out=rows_a[:], in_=wd_rows[0:P, :])
        nc.sync.dma_start(out=xs[:, 2:4, :], in_=x_tiles[:, 2:4, :])
        nc.sync.dma_start(out=xs[:, 4:TILES, :], in_=x_tiles[:, 4:TILES, :])
        nc.sync.dma_start(out=w1_first[:].bitcast(I32), in_=w1_branches[:, :, 0:W1_BYTES].bitcast(I32))
        for quad in range(QUADS):
            nc.sync.dma_start(
                out=w1s[32 * quad : 32 * quad + 4, :].bitcast(I32),
                in_=w1_scales[0, 4 * quad : 4 * quad + 4, :].bitcast(I32),
            )
        nc.sync.dma_start(out=w1_rest[:].bitcast(I32), in_=w1_branches[:, :, W1_BYTES:].bitcast(I32))

        nc.vector.tensor_copy(out=ident_bf[:], in_=ident[:])
        nc.vector.tensor_copy(
            out=perm[:].rearrange("p (u c e) -> p u c e", u=2, e=2),
            in_=ident[:].rearrange("p (c u e) -> p u c e", u=2, e=2),
        )
        nc.vector.memset(u[:].rearrange("p b (i j) -> p b i j", j=PITCH)[:, :, :, 0:LEAD], 0.0)
        nc.vector.memset(u[:, :, PITCH * GRID + LEAD : PITCH * (GRID + 1)], 0.0)
        nc.vector.memset(top[:, 1:, 0:GRID], 0.0)
        nc.vector.memset(w2s[:].rearrange("p g n -> p (g n)").bitcast(U32), 0)
        nc.sync.dma_start(out=w2w[:].bitcast(I32), in_=w2_words.rearrange("g p n -> p g n").bitcast(I32))
        for quad in range(QUADS):
            nc.sync.dma_start(
                out=w2s[32 * quad : 32 * quad + 4, :, :].bitcast(I32),
                in_=w2_scales[:, 4 * quad : 4 * quad + 4, :].rearrange("g r n -> r g n").bitcast(I32),
            )

        def copy(engine, dst, src):
            if engine == "scalar":
                nc.scalar.copy(out=dst, in_=src)
            else:
                nc.vector.tensor_copy(out=dst, in_=src)

        def turn(index, words):
            turned = bank(index, [P, len(words), 2, P])
            for q in range(len(words)):
                for half in range(2):
                    nc.tensor.transpose(turned[:, q, half, :], words[q][half], ident[:])
            return turned

        def weave(engine, woven, turned):
            copy(
                engine,
                woven.bitcast(F32).rearrange("p (q m) u -> p q m u", m=P),
                turned[:].rearrange("p q u m -> p q m u"),
            )

        def quantize(woven, codes, scales):
            nc.vector.quantize_mx(out=codes.bitcast(FP8X4), scales=scales, in_=woven.rearrange("p m t -> p (m t)"))

        def x_turn(q0, index):
            words = [xs[:, q, :].bitcast(F32) for q in (q0, q0 + 1)]
            return turn(index, [[w[:, half : 2 * P : 2] for half in range(2)] for w in words])

        def x_quant(m0, m1):
            quantize(x_woven[:, m0:m1, :], x_codes[:, m0:m1], x_scales[:, m0:m1])

        chunk_of = [c for j in range(PAIRS) for c in (PAIRS + j, j)]
        h_banks = {}

        def expand(slot, half):
            chunk = chunk_of[slot]
            branch, j = divmod(chunk, PAIRS)
            words = w1_first[:, branch, :] if j == 0 else w1_rest[:, branch, W1_BYTES * (j - 1) : W1_BYTES * j]
            tokens = slice(HALF * half, HALF * (half + 1))
            h_banks[slot, half] = bank(2 * (slot % 2) + half, [P, HALF])
            nc.tensor.matmul_mx(
                out=h_banks[slot, half][:],
                lhsT=words.bitcast(FP4X4),
                lhsT_scale=w1s[:, P * chunk : P * (chunk + 1)],
                rhs=x_codes[:, tokens].bitcast(FP8X4),
                rhs_scale=x_scales[:, tokens],
                start=True,
                stop=True,
            )

        def window(slot, tap, i0, i1):
            first = LEAD + PITCH * (i0 + tap // 3 - 1) + tap % 3 - 1
            rows = u[:, slot % U_BUFS, first : first + PITCH * (i1 - i0)]
            return rows.rearrange("p (i j) -> p i j", j=PITCH)[:, :, 0:GRID]

        def activate(slot, half):
            col = BIAS_COL + chunk_of[slot]
            nc.scalar.activation(
                out=window(slot, 4, GRID // 2 * half, GRID // 2 * (half + 1)),
                in_=h_banks[slot, half][:].rearrange("p (i j) -> p i j", j=GRID),
                func=ACT.Silu,
                bias=cols[:, col : col + 1],
            )

        def weight(slot, tap):
            col = CHUNKS * tap + chunk_of[slot]
            return cols[:, col : col + 1]

        def grid_rows(tile, i0, i1):
            return tile[:, GRID * i0 : GRID * i1].rearrange("p (i j) -> p i j", j=GRID)

        tops_made = []

        def top_product(unit, tap):
            slot, q0, q1 = unit
            tile = top[:, len(tops_made) % TOP_BUFS, :]
            tops_made.append(tap)
            i0, i1 = max(1, ROWS * q0), ROWS * q1
            nc.scalar.activation(
                out=grid_rows(tile, i0, i1), in_=window(slot, tap, i0, i1), func=ACT.Copy, scale=weight(slot, tap)
            )
            return tile

        def product(engine, unit, tap):
            slot, q0, q1 = unit
            tile = prods.tile([P, TOK], F32, name="pr", tag="pr")
            dst, src = grid_rows(tile, ROWS * q0, ROWS * q1), window(slot, tap, ROWS * q0, ROWS * q1)
            if engine == "scalar":
                nc.scalar.activation(out=dst, in_=src, func=ACT.Copy, scale=weight(slot, tap))
            else:
                nc.vector.tensor_scalar(out=dst, in0=src, scalar1=weight(slot, tap), scalar2=None, op0=ALU.mult)
            return tile

        def add_product(unit, tap, tile):
            slot, q0, q1 = unit
            i0, i1 = ROWS * q0, min(GRID - 1, ROWS * q1)
            dst = grid_rows(tile, i0, i1)
            nc.vector.scalar_tensor_tensor(
                out=dst, in0=window(slot, tap, i0, i1), scalar=weight(slot, tap), in1=dst, op0=ALU.mult, op1=ALU.add
            )

        def spans(unit):
            slot, q0, q1 = unit
            return [(slot, q, min(q + BANK_TILES, q1)) for q in range(q0, q1, BANK_TILES)]

        c_banks = {}

        def accumulate(unit, tile, first, last):
            for span in spans(unit):
                slot, q0, q1 = span
                if first:
                    c_banks[span] = bank(SUM_BANK + len(c_banks) % 4, [P, q1 - q0, P])
                for q in range(q0, q1):
                    nc.tensor.matmul(
                        out=c_banks[span][:, q - q0, :],
                        lhsT=tile[:, P * q : P * (q + 1)],
                        rhs=perm[:],
                        is_transpose=True,
                        start=(first and q == q0),
                        stop=(last and q == q1 - 1),
                    )

        silu_cb = {}

        def drain(unit):
            for span in spans(unit):
                slot, q0, q1 = span
                if slot % 2 == 0:
                    gate = gates.tile([P, q1 - q0, P], F32, name="gate", tag="gate")
                    nc.scalar.activation(out=gate[:], in_=c_banks[span][:], func=ACT.Silu)
                    for q in range(q0, q1):
                        silu_cb[q] = (gate, q0)
                else:
                    group, j = divmod(chunk_of[slot], 4)
                    gate, base = silu_cb[q0]
                    nc.vector.tensor_tensor(
                        out=g_tok[:, q0:q1, group, :, P // 2 * j : P // 2 * (j + 1)],
                        in0=c_banks[span][:].rearrange("p q (u c) -> p q u c", u=2),
                        in1=gate[:, q0 - base : q1 - base, :].rearrange("p q (u c) -> p q u c", u=2),
                        op=ALU.mult,
                    )

        g_turned, o_turned, o_banks, o32, o16 = {}, {}, {}, {}, {}

        def g_turn(group, q0, index, n=2):
            words = [[g_tok[:, q, group, half, :].bitcast(F32) for half in range(2)] for q in range(q0, q0 + n)]
            g_turned[q0] = turn(index, words)

        def g_weave(group, q0, n=2):
            weave("scalar", g_woven[:, group, P * q0 : P * (q0 + n), :], g_turned[q0])

        def g_quant(group, q0, q1):
            tokens = slice(P * q0, P * q1)
            quantize(g_woven[:, group, tokens, :], g_codes[:, group, tokens], g_scales[:, group, tokens])

        def project(q, index):
            o_banks[q] = bank(index, [P, D])
            for group in range(2):
                nc.tensor.matmul_mx(
                    out=o_banks[q][:],
                    lhsT=g_codes[:, group, P * q : P * (q + 1)].bitcast(FP8X4),
                    lhsT_scale=g_scales[:, group, P * q : P * (q + 1)],
                    rhs=w2w[:, group, :].bitcast(FP4X4),
                    rhs_scale=w2s[:, group, :],
                    start=(group == 0),
                    stop=(group == 1),
                )

        def evacuate(q, engine="scalar"):
            o32[q] = outs.tile([P, D], F32, name="o32", tag="o32")
            copy(engine, o32[q][:], o_banks[q][:])
            nc.sync.dma_start(out=out_rows[P * q : P * (q + 1), :], in_=o32[q][:])

        def narrow(q, engine="vector", source=o32):
            o16[q] = outs.tile([P, 2, 2 * P], BF16, name="o16", tag="o16")
            copy(
                engine,
                o16[q][:].rearrange("p u (c e) -> p u c e", e=2),
                source[q][:].rearrange("p (c u e) -> p u c e", u=2, e=2),
            )

        def o_turn(q0, index, n=2):
            o_turned[q0] = turn(index, [[o16[q][:, half, :].bitcast(F32) for half in range(2)] for q in range(q0, q0 + n)])

        def o_weave(q0, engine, n=2):
            weave(engine, o_woven[:, P * q0 : P * (q0 + n), :], o_turned[q0])

        def o_quant(q0, q1):
            tokens = slice(P * q0, P * q1)
            quantize(o_woven[:, tokens, :], o_codes[:, tokens], o_scales[:, tokens])
            nc.sync.dma_start(out=out_words[:, tokens], in_=o_codes[:, tokens].bitcast(I32))

        x_turned = [x_turn(0, SUM_BANK)]
        cols_bank = bank(3, [P, 2, P], BF16)
        nc.tensor.transpose(cols_bank[:, 1, :], rows_b[:], ident_bf[:])
        nc.tensor.transpose(cols_bank[:, 0, :], rows_a[:], ident_bf[:])
        x_turned += [x_turn(2 * r, SUM_BANK + r) for r in range(1, 4)]
        weave("vector", x_woven[:, 0 : 2 * P, :], x_turned[0])
        weave("scalar", x_woven[:, 2 * P : HALF, :], x_turned[1])
        nc.vector.tensor_copy(out=cols[:], in_=cols_bank[:].rearrange("p a c -> p (a c)"))
        x_quant(0, 2 * P)
        linear_taps = cols[:, 0:BIAS_COL].rearrange("p (k m) -> p k m", m=CHUNKS)[:, :, 0:PAIRS]
        nc.vector.tensor_tensor(
            out=linear_taps,
            in0=linear_taps,
            in1=cols[:, GAIN_COL : GAIN_COL + PAIRS].unsqueeze(1).to_broadcast([P, TAPS, PAIRS]),
            op=ALU.mult,
        )
        x_quant(2 * P, HALF)
        expand(0, 0)
        expand(1, 0)
        weave("scalar", x_woven[:, HALF : HALF + 2 * P, :], x_turned[2])
        weave("vector", x_woven[:, HALF + 2 * P : TOK, :], x_turned[3])
        activate(0, 0)
        x_quant(HALF, TOK)

        units = [(0, 0, 3), (1, 0, 3), (0, 3, TILES), (1, 3, TILES)]
        units += [(slot, 0, TILES) for slot in range(2, CHUNKS - 4)]
        units += [(slot, 0, 4) for slot in range(CHUNKS - 4, CHUNKS)]
        second = len(units)
        units += [(slot, 4, TILES) for slot in range(CHUNKS - 4, CHUNKS - 1)]
        units += [(CHUNKS - 1, 4, 6), (CHUNKS - 1, 6, TILES)]

        placed = {}

        def place(n, mark, step, *args):
            placed.setdefault((n, mark), []).append((step, args))

        def run(n, mark):
            for step, args in placed.get((n, mark), []):
                step(*args)

        place(0, "s_early", activate, 1, 0)
        place(0, "t_early", expand, 0, 1)
        place(0, "t_early", expand, 1, 1)
        place(0, "s_late", activate, 0, 1)
        place(1, "s_early", activate, 1, 1)
        for slot in range(2, CHUNKS):
            for half in range(2):
                place(slot - slot % 2 - 1, "t_late", expand, slot, half)
                place(slot, "s_late", activate, slot, half)
        for half in range(2):
            n = 11 + 2 * half
            for k in range(2):
                place(n, "t_early", g_turn, 0, 4 * half + 2 * k, k)
                place(n, "s_late", g_weave, 0, 4 * half + 2 * k)
            place(n + 1, "v_late", g_quant, 0, 4 * half, 4 * half + 4)
        for k in range(2):
            place(second, "t_late", g_turn, 1, 2 * k, k)
            place(second + 1, "s_late", g_weave, 1, 2 * k)
        place(second + 2, "v_mid", g_quant, 1, 0, 4)
        for q in range(4):
            place(second + 2, "t_early", project, q, (q + 2) % 4)
        for q in range(2):
            place(second + 2, "s_late", evacuate, q)
            place(second + 3, "v_late", narrow, q)
            place(second + 4, "s_late", evacuate, q + 2)
        place(second + 3, "t_late", o_turn, 0, 2)
        place(second + 4, "t_late", g_turn, 1, 4, 3)

        for n, unit in enumerate(units):
            slot, q0, q1 = unit
            n_added = 3 if (slot % 2 == 1 and q1 - q0 == TILES) or n >= second else 2
            scalar_takes_5 = n >= len(units) - 3
            vector_taps = ([3, 4] if scalar_takes_5 else [3, 4, 5]) + list(range(6, TAPS - n_added))

            top0 = top_product(unit, 0)
            made = [product("vector", unit, tap) for tap in vector_taps]
            run(n, "s_early")
            run(n, "v_mid")
            top1 = top_product(unit, 1)
            top2 = top_product(unit, 2)
            fifth = [product("scalar", unit, 5)] if scalar_takes_5 else []
            for k in range(n_added):
                add_product(unit, TAPS - n_added + k, made[k % len(made)])
            if n == len(units) - 1:
                drain(units[n - 2])
            if n > 0 and n != len(units) - 2:
                drain(units[n - 1])
            run(n, "v_late")
            plain = made[n_added:]
            added = [made[k % len(made)] for k in range(n_added)][-len(made) :]
            tiles = plain[:1] + [top0] + plain[1:] + [top1] + added[:1] + [top2] + added[1:] + fifth
            for k, tile in enumerate(tiles):
                if k == 2:
                    run(n, "t_early")
                accumulate(unit, tile, k == 0, k == len(tiles) - 1)
            run(n, "s_late")
            run(n, "t_late")

        drain(units[-1])
        g_turn(1, 6, 6, 1)
        g_weave(1, 4)
        g_weave(1, 6, 1)
        g_turn(1, 7, 7, 1)
        g_quant(1, 4, 6)
        narrow(2)
        g_weave(1, 7, 1)
        project(4, 4)
        g_quant(1, 6, TILES)
        evacuate(4)
        narrow(3)
        o_weave(0, "vector")
        project(5, 5)
        project(6, 1)
        evacuate(5, "vector")
        narrow(4)
        evacuate(6)
        o_turn(2, 0)
        narrow(5)
        narrow(6)
        o_weave(2, "scalar")
        project(7, 6)
        o_turn(4, 3)
        o_turn(6, 4, 1)
        o_quant(0, 4)
        narrow(7, "scalar", o_banks)
        evacuate(7)
        o_turn(7, 7, 1)
        o_weave(6, "vector", 1)
        o_weave(7, "vector", 1)
        o_quant(6, TILES)
        o_weave(4, "scalar")
        o_quant(4, 6)
        for quad in range(QUADS):
            nc.scalar.dma_start(
                out=out_2[0, 4 * quad : 4 * quad + 4, :].bitcast(I32),
                in_=o_scales[32 * quad : 32 * quad + 4, :].bitcast(I32),
            )
